import numpy as np
import ml_dtypes


def mxq(x, axis, fmt="e4m3"):
    dtype, down = {"e4m3": (ml_dtypes.float8_e4m3fn, 7), "e5m2": (ml_dtypes.float8_e5m2, 14)}[fmt]
    v = np.moveaxis(np.asarray(x, np.float32).astype(ml_dtypes.bfloat16).astype(np.float64), axis, -1)
    blocks = v.reshape(v.shape[:-1] + (-1, 32))
    amax = np.abs(blocks).max(-1, keepdims=True)
    byte = np.maximum(np.where(amax > 0, np.frexp(amax)[1] - 1 + 127, 0) - down, 1)
    scale = np.exp2(byte - 127.0)
    codes = (blocks / scale).astype(np.float32).astype(dtype).astype(np.float64)
    return np.moveaxis((codes * scale).reshape(v.shape), -1, axis)


WIDE = False


def mx_kscale(k):
    if not WIDE:
        return np.ones(k)
    levels = np.array([30, -30])
    if k % 512:
        return np.exp2(np.random.permutation(np.resize(levels, k // 32))).repeat(32)
    a = np.empty((k // 512, 16))
    for p in range(k // 512):
        a[p, :8] = np.random.permutation(np.resize(levels, 8))
        for g in range(8):
            far = levels[np.abs(levels - a[p, g]) >= 10]
            a[p, g + 8] = far[np.random.randint(len(far))]
    return np.exp2(a.ravel()).repeat(32)


def f64(x):
    return np.asarray(x).astype(np.float64)


def striped(idx):
    return np.tile(np.asarray(idx).reshape(-1, 16).T, (8, 1)).astype(np.uint16)


def unstriped(offs):
    return offs[:16].T.reshape(-1).astype(np.int64)


E2M1 = np.array([0.0, 0.5, 1.0, 1.5, 2.0, 3.0, 4.0, 6.0, -0.0, -0.5, -1.0, -1.5, -2.0, -3.0, -4.0, -6.0])


def pack_weight(w, fmt):
    k, n = w.shape
    w = f64(np.asarray(w, np.float32).astype(ml_dtypes.bfloat16)).reshape(k // 32, 32, n)
    amax = np.abs(w).max(1)
    if fmt in ("e4m3", "e5m2"):
        byte = np.frexp(amax)[1] - 1 + 127 - (7 if fmt == "e4m3" else 14)
    else:
        mant, ex = np.frexp(amax / 6.0)
        byte = np.where(mant > 0.5, ex, ex - 1) + 127
    byte = np.clip(np.where(amax > 0, byte, 1), 1, 254)
    scaled = (w * np.exp2(127.0 - byte)[:, None, :]).reshape(k, n).astype(np.float32)
    by_word = np.ascontiguousarray(scaled.reshape(k // 512, 128, 4, n).transpose(0, 1, 3, 2))
    if fmt in ("e4m3", "e5m2"):
        words = by_word.astype(ml_dtypes.float8_e4m3fn if fmt == "e4m3" else ml_dtypes.float8_e5m2).view(np.uint8)
    else:
        c = by_word.astype(ml_dtypes.float4_e2m1fn).view(np.uint8) & 0xF
        words = (c[..., 0::2] | (c[..., 1::2] << 4)).reshape(k // 512, 128, 2 * n)
    return np.ascontiguousarray(words), np.ascontiguousarray(byte.astype(np.uint8).reshape(k // 512, 16, n))


def unpack_weight(words, scales, fmt):
    g, _, n = scales.shape
    words = np.ascontiguousarray(words).reshape(g, 128, n, -1)
    if fmt in ("e4m3", "e5m2"):
        vals = words.view(ml_dtypes.float8_e4m3fn if fmt == "e4m3" else ml_dtypes.float8_e5m2).astype(np.float64)
    else:
        nib = np.empty((g, 128, n, 4), np.uint8)
        nib[..., 0::2] = words & 0xF
        nib[..., 1::2] = words >> 4
        vals = E2M1[nib]
    vals = vals * np.repeat(np.exp2(scales.astype(np.float64) - 127.0), 8, axis=1)[..., None]
    return vals.transpose(0, 1, 3, 2).reshape(g * 512, n)


K, T, J, R, V, C, O, N, S = 512, 1024, 256, 512, 1024, 512, 128, 256, 1024


def setup_inputs():
    n = np.random.standard_normal
    idx = np.random.permutation(V)[:R]
    idx2 = np.random.permutation(T)[:J]
    idx3 = np.random.permutation(C)[:J]
    idx4 = np.random.permutation(C)[:C]
    idx5 = np.random.permutation(C)[:O]
    idx6 = np.random.permutation(J)[:O]
    idx7 = np.random.permutation(S)[:N]
    fk = mx_kscale(K)
    fr = mx_kscale(R)
    tr = np.ones(V)
    tr[idx] = fr
    xtp = pack_weight(n((K, T)) / fk[:, None], "e5m2")
    wtp = pack_weight(n((K, V)) * 1 / np.sqrt(K) * fk[:, None] * tr, "e2m1")
    w2p = pack_weight(n((K, R)) * 1 / np.sqrt(K) * fk[:, None], "e4m3")
    vsp = pack_weight(n((R, S)) * 1 / np.sqrt(R) / fr[:, None], "e2m1")
    return {
        "xt_words": xtp[0],
        "xt_scales": xtp[1],
        "wt_words": wtp[0],
        "wt_scales": wtp[1],
        "w2_words": w2p[0],
        "w2_scales": w2p[1],
        "vs_words": vsp[0],
        "vs_scales": vsp[1],
        "offs": striped(idx),
        "offs2": striped(idx2),
        "offs3": striped(idx3),
        "offs4": striped(idx4),
        "offs5": striped(idx5),
        "offs6": striped(idx6),
        "offs7": striped(idx7),
    }


def reference(xt_words, xt_scales, wt_words, wt_scales, w2_words, w2_scales, vs_words, vs_scales, offs, offs2, offs3, offs4, offs5, offs6, offs7):
    idx = unstriped(offs)
    idx2 = unstriped(offs2)
    idx3 = unstriped(offs3)
    idx4 = unstriped(offs4)
    idx5 = unstriped(offs5)
    idx6 = unstriped(offs6)
    idx7 = unstriped(offs7)
    xtu = unpack_weight(xt_words, xt_scales, "e5m2")
    wtu = unpack_weight(wt_words, wt_scales, "e2m1")
    w2u = unpack_weight(w2_words, w2_scales, "e4m3")
    vsu = unpack_weight(vs_words, vs_scales, "e2m1")
    wtidxg = wtu[:, idx]
    xtidx2g = xtu[:, idx2]
    a = wtidxg.T @ xtidx2g
    b = w2u.T @ xtidx2g
    lb = b[:, 0:1]
    la = a[:, 0:1]
    pw = np.zeros((R, C))
    pw[:, idx3] = a
    pg = np.maximum(pw, pw[:, idx4] * lb)
    hid = np.maximum(pg[:, idx5], b[:, idx6] * la)
    vsidx7g = vsu[:, idx7]
    hidq = mxq(hid, 0, "e4m3")
    y = vsidx7g.T @ hidq
    return y

@@ -1,0 +1,206 @@
+from contextlib import ExitStack
+
+import concourse.mybir as mybir
+
+K, T, J, R, V, C, O, N, S = 512, 1024, 256, 512, 1024, 512, 128, 256, 1024
+FLOPS = 2 * K * R * J * 2 + 2 * R * N * O
+
+F32 = mybir.dt.float32
+BF16 = mybir.dt.bfloat16
+I32 = mybir.dt.int32
+U32 = mybir.dt.uint32
+U16 = mybir.dt.uint16
+U8 = mybir.dt.uint8
+E4M3 = mybir.dt.float8_e4m3fn_x4
+E5M2 = mybir.dt.float8_e5m2_x4
+E2M1 = mybir.dt.float4_e2m1fn_x4
+COPY = mybir.ActivationFunctionType.Copy
+MAX = mybir.AluOpType.max
+
+P = 128
+PACK = 4
+
+
+def tile_list_leadladder_storeleads_store_plain_kernel(
+    tc, xt_words, xt_scales, wt_words, wt_scales, w2_words, w2_scales, vs_words, vs_scales,
+    offs, offs2, offs3, offs4, offs5, offs6, offs7, out,
+):
+    nc = tc.nc
+    with ExitStack() as ctx:
+        sb = ctx.enter_context(tc.tile_pool(name="sb", bufs=1))
+        ps = ctx.enter_context(tc.psum_pool(name="ps", bufs=1))
+
+        def sbuf(name, width, dtype):
+            return sb.tile([P, width], dtype, name=name, align_bytes=64)
+
+        def load_list(name, src):
+            tile = sbuf(name, src.shape[1], U16)
+            nc.sync.dma_start(tile[:], src)
+            return tile
+
+        def zero_plane(name, width, engine):
+            plane = sbuf(name, width, U8)
+            engine.memset(plane[:].bitcast(I32), 0)
+            return plane
+
+        def load_plane(plane, src, queue, quadrants=range(4)):
+            for q in quadrants:
+                queue.dma_start(plane[32 * q : 32 * q + 4, :].bitcast(I32), src[0, 4 * q : 4 * q + 4, :].bitcast(I32))
+
+        xt_plane = zero_plane("xt_plane", T, nc.gpsimd)
+        wt_plane = zero_plane("wt_plane", V, nc.gpsimd)
+        w2_plane = zero_plane("w2_plane", R, nc.vector)
+        vs_plane = zero_plane("vs_plane", S, nc.gpsimd)
+        pw = [sbuf("pw%d" % t, C, F32) for t in range(PACK)]
+        for t in range(PACK):
+            (nc.vector if t < 2 else nc.gpsimd).memset(pw[t][:], 0.0)
+
+        w2_rows = sb.tile([4, 4, R // 4], I32, name="w2_rows", align_bytes=64)
+        nc.sync.dma_start(w2_rows[:], w2_scales[0].bitcast(I32).rearrange("(q r) c -> r q c", r=4))
+        idx = load_list("idx", offs)
+        wt_all = sbuf("wt_all", V, U16)
+        nc.sync.dma_start(wt_all[:].bitcast(I32), wt_words[0].bitcast(I32))
+        idx2 = load_list("idx2", offs2)
+        load_plane(xt_plane, xt_scales, nc.sync, range(3))
+        xt_all = sbuf("xt_all", T, I32)
+        nc.sync.dma_start(xt_all[:], xt_words[0].rearrange("p n t -> p (n t)").bitcast(I32))
+        load_plane(xt_plane, xt_scales, nc.sync, range(3, 4))
+        w2_all = sbuf("w2_all", R, I32)
+        nc.sync.dma_start(w2_all[:], w2_words[0].rearrange("p n t -> p (n t)").bitcast(I32))
+        load_plane(wt_plane, wt_scales, nc.sync)
+        idx3 = load_list("idx3", offs3)
+        idx4 = load_list("idx4", offs4)
+        idx7 = load_list("idx7", offs7)
+        vs_all = sbuf("vs_all", S, U16)
+        nc.sync.dma_start(vs_all[:].bitcast(I32), vs_words[0].bitcast(I32))
+        load_plane(vs_plane, vs_scales, nc.sync)
+        idx6 = load_list("idx6", offs6)
+        idx5 = load_list("idx5", offs5)
+
+        w2d_plane = sbuf("w2d_plane", R, U8)
+        for q in range(4):
+            nc.vector.tensor_copy(w2_plane[32 * q : 32 * q + 4, :].bitcast(I32), w2_rows[:, q, :])
+        nc.gpsimd.tensor_copy(
+            w2d_plane[:].rearrange("p (t m) -> p t m", t=PACK),
+            w2_plane[:].rearrange("p (m t) -> p t m", t=PACK),
+        )
+
+        wg_words = sbuf("wg_words", R, U16)
+        wd_words = sbuf("wd_words", R, U16)
+        nc.vector.tensor_copy(wg_words[:], wt_all[:].indirect(idx[:]))
+        xg_words = sbuf("xg_words", J, U32)
+        xg_plane = sbuf("xg_plane", J, U8)
+        nc.vector.tensor_copy(xg_words[:], xt_all[:].bitcast(U32).indirect(idx2[:]))
+        nc.vector.tensor_copy(
+            wd_words[:].rearrange("p (t m) -> p t m", t=PACK),
+            wg_words[:].rearrange("p (m t) -> p t m", t=PACK),
+        )
+        nc.vector.tensor_copy(xg_plane[:], xt_plane[:].indirect(idx2[:]))
+
+        w2d_words = sbuf("w2d_words", R, U32)
+        nc.scalar.copy(
+            w2d_words[:].rearrange("p (t m) -> p t m", t=PACK),
+            w2_all[:].bitcast(U32).rearrange("p (m t) -> p t m", t=PACK),
+        )
+
+        wd_plane = sbuf("wd_plane", R, U8)
+        nc.vector.tensor_copy(
+            wd_plane[:].rearrange("p (t m) -> p m t", t=PACK), wt_plane[:].indirect(idx[:])
+        )
+
+        b_ps = [ps.tile([P, 2, J], F32, name="b_ps%d" % h) for h in range(2)]
+        b = [sbuf("b%d" % t, J, F32) for t in range(PACK)]
+        for t in range(PACK):
+            cols = slice(P * t, P * (t + 1))
+            nc.tensor.matmul_mx(
+                out=b_ps[t // 2][:, t % 2, :],
+                lhsT=w2d_words[:, cols].bitcast(E4M3), lhsT_scale=w2d_plane[:, cols],
+                rhs=xg_words[:].bitcast(E5M2), rhs_scale=xg_plane[:],
+                start=True, stop=True,
+            )
+        for t in range(PACK):
+            nc.scalar.activation(b[t][:], b_ps[t // 2][:, t % 2, :], COPY)
+
+        a_ps = [ps.tile([P, J], F32, name="a_ps%d" % t) for t in range(PACK)]
+        a = [sbuf("a%d" % t, J, F32) for t in range(PACK)]
+        for t in range(PACK):
+            cols = slice(P * t, P * (t + 1))
+            nc.tensor.matmul_mx(
+                out=a_ps[t][:],
+                lhsT=wd_words[:].bitcast(U8)[:, 2 * P * t : 2 * P * (t + 1)].bitcast(E2M1), lhsT_scale=wd_plane[:, cols],
+                rhs=xg_words[:].bitcast(E5M2), rhs_scale=xg_plane[:],
+                start=True, stop=True,
+            )
+
+        vg_words = sbuf("vg_words", N, U16)
+        vg_plane = sbuf("vg_plane", N, U8)
+        nc.vector.tensor_copy(vg_words[:], vs_all[:].indirect(idx7[:]))
+        nc.vector.tensor_copy(vg_plane[:], vs_plane[:].indirect(idx7[:]))
+
+        for t in range(PACK):
+            nc.scalar.copy(a[t][:], a_ps[t][:])
+
+        moved = [sbuf("moved%d" % t, C, F32) for t in range(PACK)]
+        pg = [sbuf("pg%d" % t, C, F32) for t in range(PACK)]
+        pg_pick = sbuf("pg_pick", PACK * O, F32)
+        b_pick = sbuf("b_pick", PACK * O, F32)
+
+        def put(t):
+            if t == 1:
+                nc.scalar.activation(pw[t][:].indirect(idx3[:]), a[t][:], COPY)
+            else:
+                nc.vector.tensor_copy(pw[t][:].indirect(idx3[:]), a[t][:])
+
+        def fetch(t):
+            for h in range(2):
+                nc.scalar.activation(
+                    moved[t][:, 256 * h : 256 * (h + 1)], pw[t][:].indirect(idx4[:, 16 * h : 16 * (h + 1)]),
+                    COPY, scale=b[t][:, 0:1],
+                )
+
+        def keep(t):
+            nc.vector.tensor_tensor(pg[t][:], pw[t][:], moved[t][:], MAX)
+
+        def pick_pg(t, on_vector):
+            dst = pg_pick[:, O * t : O * (t + 1)]
+            if on_vector:
+                nc.vector.tensor_copy(dst, pg[t][:].indirect(idx5[:]))
+            else:
+                nc.scalar.activation(dst, pg[t][:].indirect(idx5[:]), COPY)
+
+        def pick_b(t):
+            nc.scalar.activation(b_pick[:, O * t : O * (t + 1)], b[t][:].indirect(idx6[:]), COPY, scale=a[t][:, 0:1])
+
+        for t in range(PACK):
+            put(t)
+        for t in range(PACK):
+            fetch(t)
+            keep(t)
+        for t in range(PACK):
+            pick_b(t)
+        for t in range(PACK):
+            pick_pg(t, t >= 2)
+
+        hid = sbuf("hid", O * PACK, BF16)
+        nc.vector.tensor_tensor(
+            hid[:].rearrange("p (c i t) -> p c t i", i=4, t=PACK),
+            pg_pick[:].rearrange("p (t c i) -> p c t i", i=4, t=PACK),
+            b_pick[:].rearrange("p (t c i) -> p c t i", i=4, t=PACK),
+            MAX,
+        )
+        hid_words = sbuf("hid_words", O, U32)
+        hid_plane = sbuf("hid_plane", O, U8)
+        nc.vector.quantize_mx(out=hid_words[:].bitcast(E4M3), scales=hid_plane[:], in_=hid[:])
+
+        y_ps = ps.tile([P, 2, O], F32, name="y_ps")
+        for h in range(2):
+            nc.tensor.matmul_mx(
+                out=y_ps[:, h, :],
+                lhsT=vg_words[:].bitcast(U8)[:, 2 * P * h : 2 * P * (h + 1)].bitcast(E2M1),
+                lhsT_scale=vg_plane[:, P * h : P * (h + 1)],
+                rhs=hid_words[:].bitcast(E4M3), rhs_scale=hid_plane[:],
+                start=True, stop=True,
+            )
+        y = sb.tile([P, 2, O], F32, name="y")
+        nc.vector.tensor_copy(y[:], y_ps[:])
+        nc.sync.dma_start(out.rearrange("(h p) o -> p h o", h=2), y[:])

@@ -30,8 +30,8 @@ def tile_list_leadladder_storeleads_store_plain_kernel(
         sb = ctx.enter_context(tc.tile_pool(name="sb", bufs=1))
         ps = ctx.enter_context(tc.psum_pool(name="ps", bufs=1))
 
-        def sbuf(name, width, dtype):
-            return sb.tile([P, width], dtype, name=name, align_bytes=64)
+        def sbuf(name, width, dtype, tag=None):
+            return sb.tile([P, width], dtype, name=name, tag=tag or name, align_bytes=64)
 
         def load_list(name, src):
             tile = sbuf(name, src.shape[1], U16)
@@ -48,78 +48,60 @@ def tile_list_leadladder_storeleads_store_plain_kernel(
                 queue.dma_start(plane[32 * q : 32 * q + 4, :].bitcast(I32), src[0, 4 * q : 4 * q + 4, :].bitcast(I32))
 
         xt_plane = zero_plane("xt_plane", T, nc.gpsimd)
-        wt_plane = zero_plane("wt_plane", V, nc.gpsimd)
-        w2_plane = zero_plane("w2_plane", R, nc.vector)
-        vs_plane = zero_plane("vs_plane", S, nc.gpsimd)
-        pw = [sbuf("pw%d" % t, C, F32) for t in range(PACK)]
+        w2_plane = zero_plane("w2_plane", R, nc.gpsimd)
+        wt_plane = zero_plane("wt_plane", V, nc.vector)
+        pw = [sbuf("pw%d" % t, 2 * C, F32) for t in range(PACK)]
         for t in range(PACK):
-            (nc.vector if t < 2 else nc.gpsimd).memset(pw[t][:], 0.0)
+            (nc.vector if t < 3 else nc.gpsimd).memset(pw[t][:, :C], 0.0)
+        vs_plane = zero_plane("vs_plane", S, nc.vector)
 
-        w2_rows = sb.tile([4, 4, R // 4], I32, name="w2_rows", align_bytes=64)
-        nc.sync.dma_start(w2_rows[:], w2_scales[0].bitcast(I32).rearrange("(q r) c -> r q c", r=4))
+        idx2 = load_list("idx2", offs2)
+        load_plane(xt_plane, xt_scales, nc.sync)
         idx = load_list("idx", offs)
         wt_all = sbuf("wt_all", V, U16)
         nc.sync.dma_start(wt_all[:].bitcast(I32), wt_words[0].bitcast(I32))
-        idx2 = load_list("idx2", offs2)
-        load_plane(xt_plane, xt_scales, nc.sync, range(3))
         xt_all = sbuf("xt_all", T, I32)
         nc.sync.dma_start(xt_all[:], xt_words[0].rearrange("p n t -> p (n t)").bitcast(I32))
-        load_plane(xt_plane, xt_scales, nc.sync, range(3, 4))
+        load_plane(wt_plane, wt_scales, nc.sync)
         w2_all = sbuf("w2_all", R, I32)
         nc.sync.dma_start(w2_all[:], w2_words[0].rearrange("p n t -> p (n t)").bitcast(I32))
-        load_plane(wt_plane, wt_scales, nc.sync)
-        idx3 = load_list("idx3", offs3)
-        idx4 = load_list("idx4", offs4)
         idx7 = load_list("idx7", offs7)
         vs_all = sbuf("vs_all", S, U16)
         nc.sync.dma_start(vs_all[:].bitcast(I32), vs_words[0].bitcast(I32))
-        load_plane(vs_plane, vs_scales, nc.sync)
+        idx3 = load_list("idx3", offs3)
+        load_plane(w2_plane, w2_scales, nc.sync)
+        idx4 = load_list("idx4", offs4)
         idx6 = load_list("idx6", offs6)
+        load_plane(vs_plane, vs_scales, nc.sync)
         idx5 = load_list("idx5", offs5)
 
-        w2d_plane = sbuf("w2d_plane", R, U8)
-        for q in range(4):
-            nc.vector.tensor_copy(w2_plane[32 * q : 32 * q + 4, :].bitcast(I32), w2_rows[:, q, :])
-        nc.gpsimd.tensor_copy(
-            w2d_plane[:].rearrange("p (t m) -> p t m", t=PACK),
-            w2_plane[:].rearrange("p (m t) -> p t m", t=PACK),
-        )
-
-        wg_words = sbuf("wg_words", R, U16)
-        wd_words = sbuf("wd_words", R, U16)
-        nc.vector.tensor_copy(wg_words[:], wt_all[:].indirect(idx[:]))
         xg_words = sbuf("xg_words", J, U32)
         xg_plane = sbuf("xg_plane", J, U8)
+        wg_words = sbuf("wg_words", R, U16)
+        wd_words = sbuf("wd_words", R, U16, tag="wt_plane")
+        wd_plane = sbuf("wd_plane", R, U8)
+        nc.vector.tensor_copy(xg_plane[:], xt_plane[:].indirect(idx2[:]))
+        nc.vector.tensor_copy(wg_words[:], wt_all[:].indirect(idx[:]))
         nc.vector.tensor_copy(xg_words[:], xt_all[:].bitcast(U32).indirect(idx2[:]))
         nc.vector.tensor_copy(
-            wd_words[:].rearrange("p (t m) -> p t m", t=PACK),
-            wg_words[:].rearrange("p (m t) -> p t m", t=PACK),
+            wd_plane[:].rearrange("p (t m) -> p m t", t=PACK), wt_plane[:].indirect(idx[:])
         )
-        nc.vector.tensor_copy(xg_plane[:], xt_plane[:].indirect(idx2[:]))
+        for half in range(2):
+            nc.vector.tensor_copy(
+                wd_words[:].rearrange("p (t m) -> p t m", t=PACK)[:, 2 * half : 2 * half + 2, :],
+                wg_words[:].rearrange("p (m t) -> p t m", t=PACK)[:, 2 * half : 2 * half + 2, :],
+            )
 
         w2d_words = sbuf("w2d_words", R, U32)
+        w2d_plane = sbuf("w2d_plane", R, U8)
         nc.scalar.copy(
             w2d_words[:].rearrange("p (t m) -> p t m", t=PACK),
             w2_all[:].bitcast(U32).rearrange("p (m t) -> p t m", t=PACK),
         )
-
-        wd_plane = sbuf("wd_plane", R, U8)
-        nc.vector.tensor_copy(
-            wd_plane[:].rearrange("p (t m) -> p m t", t=PACK), wt_plane[:].indirect(idx[:])
+        nc.gpsimd.tensor_copy(
+            w2d_plane[:].rearrange("p (t m) -> p t m", t=PACK),
+            w2_plane[:].rearrange("p (m t) -> p t m", t=PACK),
         )
-
-        b_ps = [ps.tile([P, 2, J], F32, name="b_ps%d" % h) for h in range(2)]
-        b = [sbuf("b%d" % t, J, F32) for t in range(PACK)]
-        for t in range(PACK):
-            cols = slice(P * t, P * (t + 1))
-            nc.tensor.matmul_mx(
-                out=b_ps[t // 2][:, t % 2, :],
-                lhsT=w2d_words[:, cols].bitcast(E4M3), lhsT_scale=w2d_plane[:, cols],
-                rhs=xg_words[:].bitcast(E5M2), rhs_scale=xg_plane[:],
-                start=True, stop=True,
-            )
-        for t in range(PACK):
-            nc.scalar.activation(b[t][:], b_ps[t // 2][:, t % 2, :], COPY)
 
         a_ps = [ps.tile([P, J], F32, name="a_ps%d" % t) for t in range(PACK)]
         a = [sbuf("a%d" % t, J, F32) for t in range(PACK)]
@@ -131,35 +113,30 @@ def tile_list_leadladder_storeleads_store_plain_kernel(
                 rhs=xg_words[:].bitcast(E5M2), rhs_scale=xg_plane[:],
                 start=True, stop=True,
             )
-
-        vg_words = sbuf("vg_words", N, U16)
-        vg_plane = sbuf("vg_plane", N, U8)
-        nc.vector.tensor_copy(vg_words[:], vs_all[:].indirect(idx7[:]))
-        nc.vector.tensor_copy(vg_plane[:], vs_plane[:].indirect(idx7[:]))
-
+        b_ps = [ps.tile([P, 2, J], F32, name="b_ps%d" % h) for h in range(2)]
+        b = [sbuf("b%d" % t, J, F32) for t in range(PACK)]
         for t in range(PACK):
-            nc.scalar.copy(a[t][:], a_ps[t][:])
+            cols = slice(P * t, P * (t + 1))
+            nc.tensor.matmul_mx(
+                out=b_ps[t // 2][:, t % 2, :],
+                lhsT=w2d_words[:, cols].bitcast(E4M3), lhsT_scale=w2d_plane[:, cols],
+                rhs=xg_words[:].bitcast(E5M2), rhs_scale=xg_plane[:],
+                start=True, stop=True,
+            )
 
         moved = [sbuf("moved%d" % t, C, F32) for t in range(PACK)]
         pg = [sbuf("pg%d" % t, C, F32) for t in range(PACK)]
         pg_pick = sbuf("pg_pick", PACK * O, F32)
         b_pick = sbuf("b_pick", PACK * O, F32)
-
-        def put(t):
-            if t == 1:
-                nc.scalar.activation(pw[t][:].indirect(idx3[:]), a[t][:], COPY)
-            else:
-                nc.vector.tensor_copy(pw[t][:].indirect(idx3[:]), a[t][:])
+        vg_words = sbuf("vg_words", N, U16)
+        vg_plane = sbuf("vg_plane", N, U8)
 
         def fetch(t):
-            for h in range(2):
-                nc.scalar.activation(
-                    moved[t][:, 256 * h : 256 * (h + 1)], pw[t][:].indirect(idx4[:, 16 * h : 16 * (h + 1)]),
-                    COPY, scale=b[t][:, 0:1],
-                )
+            nc.scalar.copy(b[t][:], b_ps[t // 2][:, t % 2, :])
+            nc.scalar.activation(moved[t][:], pw[t][:].indirect(idx4[:]), COPY, scale=b[t][:, 0:1])
 
         def keep(t):
-            nc.vector.tensor_tensor(pg[t][:], pw[t][:], moved[t][:], MAX)
+            nc.vector.tensor_tensor(pg[t][:], pw[t][:, :C], moved[t][:], MAX)
 
         def pick_pg(t, on_vector):
             dst = pg_pick[:, O * t : O * (t + 1)]
@@ -171,15 +148,23 @@ def tile_list_leadladder_storeleads_store_plain_kernel(
         def pick_b(t):
             nc.scalar.activation(b_pick[:, O * t : O * (t + 1)], b[t][:].indirect(idx6[:]), COPY, scale=a[t][:, 0:1])
 
-        for t in range(PACK):
-            put(t)
+        nc.vector.tensor_copy(vg_words[:], vs_all[:].indirect(idx7[:]))
+        nc.scalar.activation(a[0][:], a_ps[0][:], COPY)
+        nc.vector.tensor_copy(a[1][:], a_ps[1][:])
+        nc.scalar.activation(pw[0][:].indirect(idx3[:]), a[0][:], COPY)
+        nc.vector.tensor_copy(pw[1][:].indirect(idx3[:]), a[1][:])
+        nc.vector.tensor_copy(a[2][:], a_ps[2][:])
+        nc.scalar.copy(a[3][:], a_ps[3][:])
+        nc.vector.tensor_copy(pw[2][:].indirect(idx3[:]), a[2][:])
+        nc.vector.tensor_copy(pw[3][:].indirect(idx3[:]), a[3][:])
+        nc.vector.tensor_copy(vg_plane[:], vs_plane[:].indirect(idx7[:]))
         for t in range(PACK):
             fetch(t)
             keep(t)
         for t in range(PACK):
             pick_b(t)
         for t in range(PACK):
-            pick_pg(t, t >= 2)
+            pick_pg(t, True)
 
         hid = sbuf("hid", O * PACK, BF16)
         nc.vector.tensor_tensor(
@@ -192,15 +177,17 @@ def tile_list_leadladder_storeleads_store_plain_kernel(
         hid_plane = sbuf("hid_plane", O, U8)
         nc.vector.quantize_mx(out=hid_words[:].bitcast(E4M3), scales=hid_plane[:], in_=hid[:])
 
-        y_ps = ps.tile([P, 2, O], F32, name="y_ps")
+        y_ps = [ps.tile([P, O], F32, name="y_ps%d" % h) for h in range(2)]
+        y = [sbuf("y%d" % h, O, F32) for h in range(2)]
         for h in range(2):
             nc.tensor.matmul_mx(
-                out=y_ps[:, h, :],
+                out=y_ps[h][:],
                 lhsT=vg_words[:].bitcast(U8)[:, 2 * P * h : 2 * P * (h + 1)].bitcast(E2M1),
                 lhsT_scale=vg_plane[:, P * h : P * (h + 1)],
                 rhs=hid_words[:].bitcast(E4M3), rhs_scale=hid_plane[:],
                 start=True, stop=True,
             )
-        y = sb.tile([P, 2, O], F32, name="y")
-        nc.vector.tensor_copy(y[:], y_ps[:])
-        nc.sync.dma_start(out.rearrange("(h p) o -> p h o", h=2), y[:])
+        nc.vector.tensor_copy(y[0][:], y_ps[0][:])
+        nc.sync.dma_start(out[:P, :], y[0][:])
+        nc.scalar.copy(y[1][:], y_ps[1][:])
+        nc.scalar.dma_start(out[P:, :], y[1][:])

from contextlib import ExitStack

import concourse.mybir as mybir

K, T, J, R, V, C, O, N, S = 512, 1024, 256, 512, 1024, 512, 128, 256, 1024
FLOPS = 2 * K * R * J * 2 + 2 * R * N * O

F32 = mybir.dt.float32
BF16 = mybir.dt.bfloat16
I32 = mybir.dt.int32
U32 = mybir.dt.uint32
U16 = mybir.dt.uint16
U8 = mybir.dt.uint8
E4M3 = mybir.dt.float8_e4m3fn_x4
E5M2 = mybir.dt.float8_e5m2_x4
E2M1 = mybir.dt.float4_e2m1fn_x4
COPY = mybir.ActivationFunctionType.Copy
MAX = mybir.AluOpType.max

P = 128
PACK = 4


def tile_list_leadladder_storeleads_store_plain_kernel(
    tc, xt_words, xt_scales, wt_words, wt_scales, w2_words, w2_scales, vs_words, vs_scales,
    offs, offs2, offs3, offs4, offs5, offs6, offs7, out,
):
    nc = tc.nc
    with ExitStack() as ctx:
        sb = ctx.enter_context(tc.tile_pool(name="sb", bufs=1))
        ps = ctx.enter_context(tc.psum_pool(name="ps", bufs=1))

        def sbuf(name, width, dtype, tag=None):
            return sb.tile([P, width], dtype, name=name, tag=tag or name, align_bytes=64)

        def load_list(name, src):
            tile = sbuf(name, src.shape[1], U16)
            nc.sync.dma_start(tile[:], src)
            return tile

        def zero_plane(name, width, engine):
            plane = sbuf(name, width, U8)
            engine.memset(plane[:].bitcast(I32), 0)
            return plane

        def load_plane(plane, src, queue, quadrants=range(4)):
            for q in quadrants:
                queue.dma_start(plane[32 * q : 32 * q + 4, :].bitcast(I32), src[0, 4 * q : 4 * q + 4, :].bitcast(I32))

        xt_plane = zero_plane("xt_plane", T, nc.gpsimd)
        w2_plane = zero_plane("w2_plane", R, nc.gpsimd)
        wt_plane = zero_plane("wt_plane", V, nc.vector)
        pw = [sbuf("pw%d" % t, 2 * C, F32) for t in range(PACK)]
        for t in range(PACK):
            (nc.vector if t < 3 else nc.gpsimd).memset(pw[t][:, :C], 0.0)
        vs_plane = zero_plane("vs_plane", S, nc.vector)

        idx2 = load_list("idx2", offs2)
        load_plane(xt_plane, xt_scales, nc.sync)
        idx = load_list("idx", offs)
        wt_all = sbuf("wt_all", V, U16)
        nc.sync.dma_start(wt_all[:].bitcast(I32), wt_words[0].bitcast(I32))
        xt_all = sbuf("xt_all", T, I32)
        nc.sync.dma_start(xt_all[:], xt_words[0].rearrange("p n t -> p (n t)").bitcast(I32))
        load_plane(wt_plane, wt_scales, nc.sync)
        w2_all = sbuf("w2_all", R, I32)
        nc.sync.dma_start(w2_all[:], w2_words[0].rearrange("p n t -> p (n t)").bitcast(I32))
        idx7 = load_list("idx7", offs7)
        vs_all = sbuf("vs_all", S, U16)
        nc.sync.dma_start(vs_all[:].bitcast(I32), vs_words[0].bitcast(I32))
        idx3 = load_list("idx3", offs3)
        load_plane(w2_plane, w2_scales, nc.sync)
        idx4 = load_list("idx4", offs4)
        idx6 = load_list("idx6", offs6)
        load_plane(vs_plane, vs_scales, nc.sync)
        idx5 = load_list("idx5", offs5)

        xg_words = sbuf("xg_words", J, U32)
        xg_plane = sbuf("xg_plane", J, U8)
        wg_words = sbuf("wg_words", R, U16)
        wd_words = sbuf("wd_words", R, U16, tag="wt_plane")
        wd_plane = sbuf("wd_plane", R, U8)
        nc.vector.tensor_copy(xg_plane[:], xt_plane[:].indirect(idx2[:]))
        nc.vector.tensor_copy(wg_words[:], wt_all[:].indirect(idx[:]))
        nc.vector.tensor_copy(xg_words[:], xt_all[:].bitcast(U32).indirect(idx2[:]))
        nc.vector.tensor_copy(
            wd_plane[:].rearrange("p (t m) -> p m t", t=PACK), wt_plane[:].indirect(idx[:])
        )
        for half in range(2):
            nc.vector.tensor_copy(
                wd_words[:].rearrange("p (t m) -> p t m", t=PACK)[:, 2 * half : 2 * half + 2, :],
                wg_words[:].rearrange("p (m t) -> p t m", t=PACK)[:, 2 * half : 2 * half + 2, :],
            )

        w2d_words = sbuf("w2d_words", R, U32)
        w2d_plane = sbuf("w2d_plane", R, U8)
        nc.scalar.copy(
            w2d_words[:].rearrange("p (t m) -> p t m", t=PACK),
            w2_all[:].bitcast(U32).rearrange("p (m t) -> p t m", t=PACK),
        )
        nc.gpsimd.tensor_copy(
            w2d_plane[:].rearrange("p (t m) -> p t m", t=PACK),
            w2_plane[:].rearrange("p (m t) -> p t m", t=PACK),
        )

        a_ps = [ps.tile([P, J], F32, name="a_ps%d" % t) for t in range(PACK)]
        a = [sbuf("a%d" % t, J, F32) for t in range(PACK)]
        for t in range(PACK):
            cols = slice(P * t, P * (t + 1))
            nc.tensor.matmul_mx(
                out=a_ps[t][:],
                lhsT=wd_words[:].bitcast(U8)[:, 2 * P * t : 2 * P * (t + 1)].bitcast(E2M1), lhsT_scale=wd_plane[:, cols],
                rhs=xg_words[:].bitcast(E5M2), rhs_scale=xg_plane[:],
                start=True, stop=True,
            )
        b_ps = [ps.tile([P, 2, J], F32, name="b_ps%d" % h) for h in range(2)]
        b = [sbuf("b%d" % t, J, F32) for t in range(PACK)]
        for t in range(PACK):
            cols = slice(P * t, P * (t + 1))
            nc.tensor.matmul_mx(
                out=b_ps[t // 2][:, t % 2, :],
                lhsT=w2d_words[:, cols].bitcast(E4M3), lhsT_scale=w2d_plane[:, cols],
                rhs=xg_words[:].bitcast(E5M2), rhs_scale=xg_plane[:],
                start=True, stop=True,
            )

        moved = [sbuf("moved%d" % t, C, F32) for t in range(PACK)]
        pg = [sbuf("pg%d" % t, C, F32) for t in range(PACK)]
        pg_pick = sbuf("pg_pick", PACK * O, F32)
        b_pick = sbuf("b_pick", PACK * O, F32)
        vg_words = sbuf("vg_words", N, U16)
        vg_plane = sbuf("vg_plane", N, U8)

        def fetch(t):
            nc.scalar.copy(b[t][:], b_ps[t // 2][:, t % 2, :])
            nc.scalar.activation(moved[t][:], pw[t][:].indirect(idx4[:]), COPY, scale=b[t][:, 0:1])

        def keep(t):
            nc.vector.tensor_tensor(pg[t][:], pw[t][:, :C], moved[t][:], MAX)

        def pick_pg(t, on_vector):
            dst = pg_pick[:, O * t : O * (t + 1)]
            if on_vector:
                nc.vector.tensor_copy(dst, pg[t][:].indirect(idx5[:]))
            else:
                nc.scalar.activation(dst, pg[t][:].indirect(idx5[:]), COPY)

        def pick_b(t):
            nc.scalar.activation(b_pick[:, O * t : O * (t + 1)], b[t][:].indirect(idx6[:]), COPY, scale=a[t][:, 0:1])

        nc.vector.tensor_copy(vg_words[:], vs_all[:].indirect(idx7[:]))
        nc.scalar.activation(a[0][:], a_ps[0][:], COPY)
        nc.vector.tensor_copy(a[1][:], a_ps[1][:])
        nc.scalar.activation(pw[0][:].indirect(idx3[:]), a[0][:], COPY)
        nc.vector.tensor_copy(pw[1][:].indirect(idx3[:]), a[1][:])
        nc.vector.tensor_copy(a[2][:], a_ps[2][:])
        nc.scalar.copy(a[3][:], a_ps[3][:])
        nc.vector.tensor_copy(pw[2][:].indirect(idx3[:]), a[2][:])
        nc.vector.tensor_copy(pw[3][:].indirect(idx3[:]), a[3][:])
        nc.vector.tensor_copy(vg_plane[:], vs_plane[:].indirect(idx7[:]))
        for t in range(PACK):
            fetch(t)
            keep(t)
        for t in range(PACK):
            pick_b(t)
        for t in range(PACK):
            pick_pg(t, True)

        hid = sbuf("hid", O * PACK, BF16)
        nc.vector.tensor_tensor(
            hid[:].rearrange("p (c i t) -> p c t i", i=4, t=PACK),
            pg_pick[:].rearrange("p (t c i) -> p c t i", i=4, t=PACK),
            b_pick[:].rearrange("p (t c i) -> p c t i", i=4, t=PACK),
            MAX,
        )
        hid_words = sbuf("hid_words", O, U32)
        hid_plane = sbuf("hid_plane", O, U8)
        nc.vector.quantize_mx(out=hid_words[:].bitcast(E4M3), scales=hid_plane[:], in_=hid[:])

        y_ps = [ps.tile([P, O], F32, name="y_ps%d" % h) for h in range(2)]
        y = [sbuf("y%d" % h, O, F32) for h in range(2)]
        for h in range(2):
            nc.tensor.matmul_mx(
                out=y_ps[h][:],
                lhsT=vg_words[:].bitcast(U8)[:, 2 * P * h : 2 * P * (h + 1)].bitcast(E2M1),
                lhsT_scale=vg_plane[:, P * h : P * (h + 1)],
                rhs=hid_words[:].bitcast(E4M3), rhs_scale=hid_plane[:],
                start=True, stop=True,
            )
        nc.vector.tensor_copy(y[0][:], y_ps[0][:])
        nc.sync.dma_start(out[:P, :], y[0][:])
        nc.scalar.copy(y[1][:], y_ps[1][:])
        nc.scalar.dma_start(out[P:, :], y[1][:])
